import numpy as np
import ml_dtypes


def mxq(x, axis, fmt="e4m3"):
    dtype, down = {"e4m3": (ml_dtypes.float8_e4m3fn, 7), "e5m2": (ml_dtypes.float8_e5m2, 14)}[fmt]
    v = np.moveaxis(np.asarray(x, np.float32).astype(ml_dtypes.bfloat16).astype(np.float64), axis, -1)
    blocks = v.reshape(v.shape[:-1] + (-1, 32))
    amax = np.abs(blocks).max(-1, keepdims=True)
    byte = np.maximum(np.where(amax > 0, np.frexp(amax)[1] - 1 + 127, 0) - down, 1)
    scale = np.exp2(byte - 127.0)
    codes = (blocks / scale).astype(np.float32).astype(dtype).astype(np.float64)
    return np.moveaxis((codes * scale).reshape(v.shape), -1, axis)


WIDE = False


def mx_kscale(k):
    if not WIDE:
        return np.ones(k)
    levels = np.array([10, -10, 5, -5, 0])
    if k % 512:
        return np.exp2(np.random.permutation(np.resize(levels, k // 32))).repeat(32)
    a = np.empty((k // 512, 16))
    for p in range(k // 512):
        a[p, :8] = np.random.permutation(np.resize(levels, 8))
        for g in range(8):
            far = levels[np.abs(levels - a[p, g]) >= 10]
            a[p, g + 8] = far[np.random.randint(len(far))]
    return np.exp2(a.ravel()).repeat(32)


BF16 = ml_dtypes.bfloat16


def bf(x):
    return np.asarray(x, np.float32).astype(BF16)


def f64(x):
    return np.asarray(x).astype(np.float64)


E2M1 = np.array([0.0, 0.5, 1.0, 1.5, 2.0, 3.0, 4.0, 6.0, -0.0, -0.5, -1.0, -1.5, -2.0, -3.0, -4.0, -6.0])


def pack_weight(w, fmt):
    k, n = w.shape
    w = f64(bf(w)).reshape(k // 32, 32, n)
    amax = np.abs(w).max(1)
    if fmt == "e4m3":
        byte = np.frexp(amax)[1] - 1 + 127 - 7
    else:
        mant, ex = np.frexp(amax / 6.0)
        byte = np.where(mant > 0.5, ex, ex - 1) + 127
    byte = np.clip(np.where(amax > 0, byte, 1), 1, 254)
    scaled = (w * np.exp2(127.0 - byte)[:, None, :]).reshape(k, n).astype(np.float32)
    by_word = np.ascontiguousarray(scaled.reshape(k // 512, 128, 4, n).transpose(0, 1, 3, 2))
    if fmt == "e4m3":
        words = by_word.astype(ml_dtypes.float8_e4m3fn).view(np.uint8)
    else:
        c = by_word.astype(ml_dtypes.float4_e2m1fn).view(np.uint8) & 0xF
        words = c[..., 0::2] | (c[..., 1::2] << 4)
    return np.ascontiguousarray(words), np.ascontiguousarray(byte.astype(np.uint8).reshape(k // 512, 16, n))


def unpack_weight(words, scales, fmt):
    g, p, n, _ = words.shape
    if fmt == "e4m3":
        vals = np.ascontiguousarray(words).view(ml_dtypes.float8_e4m3fn).astype(np.float64)
    else:
        nib = np.empty((g, p, n, 4), np.uint8)
        nib[..., 0::2] = words & 0xF
        nib[..., 1::2] = words >> 4
        vals = E2M1[nib]
    vals = vals * np.repeat(np.exp2(scales.astype(np.float64) - 127.0), 8, axis=1)[..., None]
    return vals.transpose(0, 1, 3, 2).reshape(g * 512, n)
def pack4(w):
    words, scales = pack_weight(w, "e2m1")
    return words.reshape(words.shape[0], 128, -1), scales


def unpack4(words, scales):
    return unpack_weight(words.reshape(words.shape[0], 128, -1, 2), scales, "e2m1")


def planes(Y):
    n, m = Y.shape
    b = f64(bf(Y)).reshape(n // 32, 32, m)
    amax = np.abs(b).max(1)
    byte = np.clip(np.where(amax > 0, np.frexp(amax)[1] - 1 + 127 - 7, 1), 1, 254)
    codes = (b * np.exp2(127.0 - byte)[:, None, :]).reshape(n, m).astype(np.float32).astype(ml_dtypes.float8_e4m3fn).view(np.uint8)
    words = codes.reshape(n // 512, 128, 4, m).transpose(0, 1, 3, 2)
    return np.ascontiguousarray(words), np.ascontiguousarray(byte.astype(np.uint8).reshape(n // 512, 16, m))


B, S, D, F = 2, 1024, 1536, 1024

PAD_KEEP = 0.25


def setup_inputs():
    s = mx_kscale(D)
    xt = np.random.randn(D, B * S) * s[:, None]
    x_words, x_scales = pack_weight(xt, "e4m3")
    w_key = bf(np.random.randn(D, F) / np.sqrt(D) / s[:, None])
    b_key = bf(0.4 * np.random.randn(F))
    lengths = np.random.randint(S // 2, S - S // 8, size=(B, 1))
    tail = np.where(np.arange(S)[None, :] < lengths, 1.0, PAD_KEEP)
    keep = bf(tail * np.exp(0.7 * np.random.randn(B, S)))
    return {"x_words": x_words, "x_scales": x_scales, "w_key": w_key, "b_key": b_key, "keep": keep}


def reference(x_words, x_scales, w_key, b_key, keep):
    xt = unpack_weight(x_words, x_scales, "e4m3")
    wq = mxq(f64(w_key), 0, "e4m3")
    z = (xt.T @ wq).reshape(B, S, F) + f64(b_key)
    phi = np.maximum(z, 0.0) + np.exp(np.minimum(z, 0.0))
    y = phi * f64(keep)[:, :, None]
    Y = y.transpose(1, 0, 2).reshape(S, B * F)
    words, scales = planes(Y)
    return y, words, scales

@@ -1,0 +1,324 @@
+from contextlib import ExitStack
+
+import concourse.mybir as mybir
+from concourse.masks import make_identity
+
+B, S, D, F = 2, 1024, 1536, 1024
+FLOPS = 2 * B * S * D * F
+
+F32 = mybir.dt.float32
+BF16 = mybir.dt.bfloat16
+I32 = mybir.dt.int32
+U32 = mybir.dt.uint32
+U8 = mybir.dt.uint8
+FP8X4 = mybir.dt.float8_e4m3fn_x4
+ALU = mybir.AluOpType
+ACT = mybir.ActivationFunctionType
+
+P = 128
+PACK = 4
+GROUP = P * PACK
+PASSES = D // GROUP
+GROUPS = B * S // GROUP
+HALF = 512
+HALVES = F // HALF
+TILES = HALF // P
+UNITS = GROUPS * HALVES
+MX_BANKS = 4
+RUN = 2
+TURN_LAG = 3
+MASK_LAG = 4
+MASK_MOD = 16
+MASK_AT = 4
+HEAD_V = 6
+WQ_AT = (7, 7, 7)
+PAIRS_FROM = 24
+EXP_LAG = 1
+W_AT = 4
+LAST_Q = 30
+MASK_S = (6, 30)
+TAIL_SPLIT = 48
+WARM = 4
+HEAD_TILES = 2
+MAP_LAG = 2
+HEAD_SPLIT = 192
+YG_BUFS = 4
+GY = "gpsimd"
+G_RUN_W = 1
+G_RUN_Y = 1
+
+
+def tile_linear_attention_masked_keys_g6_kernel(tc, x_words, x_scales, w_key, b_key, keep, out_0, out_1, out_2):
+    nc = tc.nc
+    with ExitStack() as ctx:
+        const = ctx.enter_context(tc.tile_pool(name="const", bufs=1))
+        work = ctx.enter_context(tc.tile_pool(name="work", bufs=1))
+        psum = ctx.enter_context(tc.psum_pool(name="psum", bufs=1))
+        ctx.enter_context(tc.manual_schedule())
+
+        ident = const.tile([P, P], F32, name="ident")
+        b_rows = const.tile([F // P, P], BF16, name="b_rows")
+        b_stage = const.tile([P, P], F32, name="b_stage")
+        b_col = const.tile([P, F // P], F32, name="b_col")
+        b_neg = const.tile([P, F // P], F32, name="b_neg")
+        b_one = const.tile([P, F // P], F32, name="b_one")
+        keep_raw = const.tile([P, GROUPS, PACK], BF16, name="keep_raw")
+        keep_col = const.tile([P, GROUPS, PACK], F32, name="keep_col")
+        warm = const.tile([P, 1], F32, name="warm")
+        warm_out = const.tile([P, 1], F32, name="warm_out")
+        xs_first = const.tile([P, PASSES, GROUP], U8, name="xs_first", align_bytes=64)
+        xs_rest = const.tile([P, PASSES, (GROUPS - 1) * GROUP], U8, name="xs_rest", align_bytes=64)
+        y_scales = const.tile([P, B * F], U8, name="y_scales", align_bytes=64)
+
+        x_sb = {}
+        w_raw = {}
+        w_grouped = {}
+        w_codes = {}
+        w_scales = {}
+        w_whole = {}
+
+        def load_x(grp, g0, g1):
+            words = const.tile([P, g1 - g0, GROUP], U32, name="x%d_%d" % (grp, g0), align_bytes=64)
+            src = x_words[g0:g1, :, grp * GROUP:(grp + 1) * GROUP, :].rearrange("g p n t -> p g (n t)")
+            nc.sync.dma_start(out=words[:].bitcast(I32), in_=src.bitcast(I32))
+            for g in range(g0, g1):
+                x_sb[grp, g] = words[:, g - g0, :]
+
+        def load_x_scales(queue, dst, c0, c1):
+            for q in range(4):
+                src = x_scales[:, 4 * q:4 * q + 4, c0:c1].rearrange("g r n -> r g n")
+                queue.dma_start(out=dst[32 * q:32 * q + 4, :, :].bitcast(I32), in_=src.bitcast(I32))
+
+        def load_w(g, f0, width):
+            w_raw[g, f0] = const.tile([P, PACK, width], BF16, name="wraw%d_%d" % (g, f0))
+            src = w_key[g * GROUP:(g + 1) * GROUP, f0:f0 + width].rearrange("(p j) f -> p j f", j=PACK)
+            nc.sync.dma_start(out=w_raw[g, f0][:], in_=src)
+
+        def interleave(engine, dst, src, run):
+            dst_v = dst.rearrange("p (c i) t -> p c t i", i=run)
+            src_v = src.rearrange("p t (c i) -> p c t i", i=run)
+            if engine == "gpsimd":
+                nc.gpsimd.tensor_scalar(out=dst_v, in0=src_v, scalar1=1.0, scalar2=0.0, op0=ALU.mult, op1=ALU.add)
+            elif engine == "scalar":
+                nc.scalar.copy(out=dst_v, in_=src_v)
+            else:
+                nc.vector.tensor_copy(out=dst_v, in_=src_v)
+
+        def group_w(g, f0, shares):
+            for engine, c0, c1 in shares:
+                if c0 == 0:
+                    w_grouped[g, f0] = const.tile([P, HALF, PACK], BF16, name="wgrp%d_%d" % (g, f0), align_bytes=64)
+                interleave(engine, w_grouped[g, f0][:, c0:c1, :], w_raw[g, f0][:, :, c0:c1], G_RUN_W if engine == "gpsimd" else 4)
+
+        def quantize_w(g, f0):
+            width = w_raw[g, f0].shape[2]
+            codes = const.tile([P, width], U32, name="wcode%d_%d" % (g, f0), align_bytes=64)
+            scales = const.tile([P, width], U8, name="wscale%d_%d" % (g, f0), align_bytes=64)
+            nc.vector.quantize_mx(out=codes[:].bitcast(FP8X4), scales=scales[:],
+                                  in_=w_grouped[g, f0][:].rearrange("p f t -> p (f t)"))
+            w_whole[g, f0] = (codes[:], scales[:])
+            for c in range(0, width, P):
+                w_codes[g, (f0 + c) // P] = codes[:, c:c + P]
+                w_scales[g, (f0 + c) // P] = scales[:, c:c + P]
+
+        acc = {}
+        clamped = {}
+        expo = {}
+        phi = {}
+        turned = {}
+        y = {}
+        y_grouped = {}
+
+        def place(n):
+            u, i = divmod(n, TILES)
+            grp, half = u % GROUPS, u // GROUPS
+            return grp, half, i
+
+        def project(n, passes):
+            grp, half, i = place(n)
+            ft = half * TILES + i
+            for g in passes:
+                if g == 0:
+                    acc[n] = psum.tile([P, GROUP], F32, name="acc", bufs=MX_BANKS)
+                if grp == 0:
+                    xs = xs_first[:, g, :]
+                else:
+                    xs = xs_rest[:, g, (grp - 1) * GROUP:grp * GROUP]
+                nc.tensor.matmul_mx(out=acc[n][:], lhsT=w_codes[g, ft].bitcast(FP8X4), lhsT_scale=w_scales[g, ft],
+                                    rhs=x_sb[grp, g].bitcast(FP8X4), rhs_scale=xs,
+                                    start=(g == 0), stop=(g == PASSES - 1))
+
+        def by_slot(n):
+            return acc[n][:].rearrange("p (m t) -> p t m", t=PACK)
+
+        def clamp(n):
+            grp, half, i = place(n)
+            ft = half * TILES + i
+            clamped[n] = work.tile([P, PACK, P], F32, name="clamped", bufs=3)
+            if n < HEAD_V:
+                nc.vector.tensor_scalar(out=clamped[n][:], in0=by_slot(n), scalar1=b_col[:, ft:ft + 1], scalar2=0.0,
+                                        op0=ALU.add, op1=ALU.min)
+            else:
+                nc.scalar.activation(out=clamped[n][:], in_=by_slot(n), func=ACT.Relu, bias=b_neg[:, ft:ft + 1], scale=-1.0)
+
+        def exponential(n):
+            expo[n] = work.tile([P, PACK, P], F32, name="expo", bufs=3)
+            nc.scalar.activation(out=expo[n][:], in_=clamped[n][:], func=ACT.Exp, scale=1.0 if n < HEAD_V else -1.0)
+
+        def feature_map(n):
+            grp, half, i = place(n)
+            ft = half * TILES + i
+            phi[n] = work.tile([P, PACK, P], F32, name="phi", bufs=10)
+            nc.vector.scalar_tensor_tensor(out=phi[n][:], in0=by_slot(n), scalar=b_one[:, ft:ft + 1], in1=expo[n][:],
+                                           op0=ALU.add, op1=ALU.max)
+
+        def turn(n):
+            turned[n] = psum.tile([P, PACK, P], F32, name="turned", bufs=8 - MX_BANKS)
+            for t in range(PACK):
+                nc.tensor.transpose(turned[n][:, t, :], phi[n][:, t, :], ident[:])
+
+        def mask(n, engine):
+            grp, half, i = place(n)
+            u = n // TILES
+            if i == 0:
+                y[u] = work.tile([P, PACK, HALF], F32, name="y", bufs=3)
+            cols = slice(i * P, (i + 1) * P)
+            if engine == "scalar":
+                for t in range(PACK):
+                    nc.scalar.activation(out=y[u][:, t, cols], in_=turned[n][:, t, :], func=ACT.Copy, scale=keep_col[:, grp, t:t + 1])
+            else:
+                nc.vector.tensor_tensor(out=y[u][:, :, cols], in0=turned[n][:],
+                                        in1=keep_col[:, grp, :].unsqueeze(2).to_broadcast([P, PACK, P]), op=ALU.mult)
+
+        def store_y(n, count):
+            grp, half, i = place(n)
+            j, g = divmod(grp, S // GROUP)
+            f0 = half * HALF + i * P
+            dst = out_0[j, g * GROUP:(g + 1) * GROUP, f0:f0 + count * P].rearrange("(p t) f -> p t f", t=PACK)
+            nc.sync.dma_start(out=dst, in_=y[n // TILES][:, :, i * P:(i + count) * P])
+
+        def group_y(n, count, c0, c1, engine):
+            i = n % TILES
+            if c0 == 0:
+                y_grouped[n] = work.tile([P, count * P, PACK], BF16, name="y_grouped", bufs=YG_BUFS, align_bytes=64)
+            interleave(engine, y_grouped[n][:, c0:c1, :], y[n // TILES][:, :, i * P + c0:i * P + c1], G_RUN_Y if engine == "gpsimd" else 2)
+
+        def quantize_y(n, count):
+            grp, half, i = place(n)
+            j, g = divmod(grp, S // GROUP)
+            c0 = j * F + half * HALF + i * P
+            codes = work.tile([P, count * P], U32, name="y_codes", bufs=4, align_bytes=64)
+            nc.vector.quantize_mx(out=codes[:].bitcast(FP8X4), scales=y_scales[4 * g:P, c0:c0 + count * P],
+                                  in_=y_grouped[n][:].rearrange("p f t -> p (f t)"))
+            dst = out_1[g, :, c0:c0 + count * P, :].rearrange("p m t -> p (m t)")
+            nc.sync.dma_start(out=dst.bitcast(I32), in_=codes[:].bitcast(I32))
+
+        def store_scales(queue, c0, c1):
+            for q in range(4):
+                queue.dma_start(out=out_2[:, 4 * q:4 * q + 4, c0:c1].bitcast(I32),
+                                    in_=y_scales[32 * q:32 * q + 8, c0:c1].bitcast(I32))
+
+        nc.vector.memset(xs_first[:].rearrange("p g n -> p (g n)").bitcast(I32), 0)
+        nc.vector.memset(warm[:], 0.0)
+        nc.vector.memset(b_stage[:], 0.0)
+        nc.vector.memset(xs_rest[:].rearrange("p g n -> p (g n)").bitcast(I32), 0)
+        nc.gpsimd.dma_start(out=b_rows[:], in_=b_key.rearrange("(i p) -> i p", p=P))
+        make_identity(nc, ident[:])
+        nc.gpsimd.dma_start(out=keep_raw[:], in_=keep.rearrange("j (g p t) -> p (j g) t", p=P, t=PACK))
+        nc.scalar.activation(out=warm_out[:], in_=warm[:], func=ACT.Exp)
+        load_w(0, 0, HALF)
+        load_x_scales(nc.sync, xs_first, 0, GROUP)
+        load_w(1, 0, HALF)
+        load_w(2, 0, HALF)
+        for g in range(PASSES):
+            load_x(0, g, g + 1)
+        load_x_scales(nc.sync, xs_rest, GROUP, GROUPS * GROUP)
+        load_x(1, 0, PASSES)
+        for g in range(PASSES):
+            load_w(g, HALF, HALF)
+        load_x(2, 0, PASSES)
+        load_x(3, 0, PASSES)
+
+        for g in range(PASSES):
+            group_w(g, 0, [("scalar", 0, HEAD_SPLIT), ("vector", HEAD_SPLIT, HALF)])
+            if g == 0:
+                nc.scalar.copy(out=b_stage[0:F // P, :], in_=b_rows[:])
+                b_turned = psum.tile([P, PACK, P], F32, name="turned", bufs=8 - MX_BANKS)
+                nc.tensor.transpose(b_turned[:, 0, :], b_stage[:], ident[:])
+            if g == 1:
+                nc.vector.tensor_copy(out=b_col[:], in_=b_turned[:, 0, 0:F // P])
+                nc.vector.tensor_scalar(out=b_neg[:], in0=b_turned[:, 0, 0:F // P], scalar1=-1.0, scalar2=None, op0=ALU.mult)
+                nc.vector.tensor_scalar(out=b_one[:], in0=b_turned[:, 0, 0:F // P], scalar1=1.0, scalar2=None, op0=ALU.add)
+            if g == 2:
+                nc.vector.tensor_copy(out=keep_col[:], in_=keep_raw[:])
+            quantize_w(g, 0)
+            if g == 0:
+                for rep in range(WARM):
+                    idle = psum.tile([P, GROUP], F32, name="acc", bufs=MX_BANKS)
+                    nc.tensor.matmul_mx(out=idle[:], lhsT=w_codes[0, 0].bitcast(FP8X4), lhsT_scale=w_scales[0, 0],
+                                        rhs=w_whole[0, 0][0].bitcast(FP8X4), rhs_scale=w_whole[0, 0][1], start=True, stop=True)
+        for g in range(PASSES):
+            for n in range(HEAD_TILES):
+                project(n, [g])
+
+        steps = UNITS * TILES
+        last_unit = steps - TILES
+        turned_upto = [0]
+        masked_upto = [0]
+
+        for n in range(steps + 16):
+            if HEAD_TILES <= n < steps:
+                project(n, range(PASSES))
+            m = n - TURN_LAG if n < steps else min(n - MAP_LAG - 1, steps - 1)
+            if m >= turned_upto[0] and ((m + 1) % RUN == 0 or n >= steps) and m - masked_upto[0] < 8 - MX_BANKS:
+                for k in range(turned_upto[0], m + 1):
+                    turn(k)
+                turned_upto[0] = m + 1
+            if n < steps:
+                clamp(n)
+            if EXP_LAG <= n < steps + EXP_LAG:
+                exponential(n - EXP_LAG)
+            if MAP_LAG <= n < steps + MAP_LAG:
+                feature_map(n - MAP_LAG)
+            if n == 0:
+                group_w(1, HALF, [("gpsimd", 0, HALF)])
+                group_w(2, HALF, [("gpsimd", 0, HALF)])
+            if n == W_AT:
+                group_w(0, HALF, [("scalar", 0, HALF // 2)])
+            if n == W_AT + 1:
+                group_w(0, HALF, [("scalar", HALF // 2, HALF)])
+            for rep in range(1 if n < steps else 2):
+                k = masked_upto[0]
+                if k < turned_upto[0] and (k <= n - MASK_LAG or n >= steps):
+                    if k % TILES == TILES - 1 and TILES <= k < last_unit:
+                        quantize_y(k + 1 - 2 * TILES, TILES)
+                        for g in range(PASSES):
+                            if k == WQ_AT[g]:
+                                quantize_w(g, HALF)
+                        if k == last_unit - 1:
+                            store_scales(nc.sync, 0, B * F - HALF)
+                    if k == LAST_Q:
+                        quantize_y(last_unit - TILES, TILES)
+                    if k == steps - 1:
+                        quantize_y(last_unit, 2)
+                    mask(k, "scalar" if k % MASK_MOD == MASK_AT or k in MASK_S else "vector")
+                    masked_upto[0] = k + 1
+                    if k < last_unit:
+                        run = TILES if k < PAIRS_FROM else 2
+                        if k % run == run - 1:
+                            store_y(k + 1 - run, run)
+                        if k % TILES == TILES - 1:
+                            group_y(k + 1 - TILES, TILES, 0, HALF, GY)
+                    elif k < steps - 1:
+                        if k == last_unit + 1:
+                            store_y(k - 1, 2)
+                        if k == last_unit + 2:
+                            store_y(k, 1)
+                        group_y(k - k % 2, 2, k % 2 * P, (k % 2 + 1) * P, "scalar")
+                    else:
+                        store_y(k, 1)
+                        group_y(k - 1, 2, P, P + TAIL_SPLIT, "scalar")
+                        group_y(k - 1, 2, P + TAIL_SPLIT, 2 * P, "vector")
+                        quantize_y(k - 1, 2)
+        assert masked_upto[0] == steps
+        store_scales(nc.scalar, B * F - HALF, B * F)

@@ -28,20 +28,19 @@ MX_BANKS = 4
 RUN = 2
 TURN_LAG = 3
 MASK_LAG = 4
-MASK_MOD = 16
-MASK_AT = 4
 HEAD_V = 6
 WQ_AT = (7, 7, 7)
 PAIRS_FROM = 24
-EXP_LAG = 1
-W_AT = 4
-LAST_Q = 30
-MASK_S = (6, 30)
-TAIL_SPLIT = 48
-WARM = 4
+W_PLAN = (("gpsimd", 0, 0, 512, 0), ("gpsimd", 1, 0, 512, 0), ("scalar", 2, 0, 256, 4), ("scalar", 2, 256, 512, 5))
+MASK_S = (9, 21)
+TAIL_SPLIT = 96
+TAIL = 3
+RUN_AT = 0
 HEAD_TILES = 2
 MAP_LAG = 2
-HEAD_SPLIT = 192
+HEAD_SPLIT = 320
+ORDER = 0
+B_AT = 1
 YG_BUFS = 4
 GY = "gpsimd"
 G_RUN_W = 1
@@ -66,8 +65,7 @@ def tile_linear_attention_masked_keys_g6_kernel(tc, x_words, x_scales, w_key, b_
         keep_col = const.tile([P, GROUPS, PACK], F32, name="keep_col")
         warm = const.tile([P, 1], F32, name="warm")
         warm_out = const.tile([P, 1], F32, name="warm_out")
-        xs_first = const.tile([P, PASSES, GROUP], U8, name="xs_first", align_bytes=64)
-        xs_rest = const.tile([P, PASSES, (GROUPS - 1) * GROUP], U8, name="xs_rest", align_bytes=64)
+        x_planes = const.tile([P, B * S], U8, name="x_planes", align_bytes=64)
         y_scales = const.tile([P, B * F], U8, name="y_scales", align_bytes=64)
 
         x_sb = {}
@@ -75,7 +73,6 @@ def tile_linear_attention_masked_keys_g6_kernel(tc, x_words, x_scales, w_key, b_
         w_grouped = {}
         w_codes = {}
         w_scales = {}
-        w_whole = {}
 
         def load_x(grp, g0, g1):
             words = const.tile([P, g1 - g0, GROUP], U32, name="x%d_%d" % (grp, g0), align_bytes=64)
@@ -83,11 +80,6 @@ def tile_linear_attention_masked_keys_g6_kernel(tc, x_words, x_scales, w_key, b_
             nc.sync.dma_start(out=words[:].bitcast(I32), in_=src.bitcast(I32))
             for g in range(g0, g1):
                 x_sb[grp, g] = words[:, g - g0, :]
-
-        def load_x_scales(queue, dst, c0, c1):
-            for q in range(4):
-                src = x_scales[:, 4 * q:4 * q + 4, c0:c1].rearrange("g r n -> r g n")
-                queue.dma_start(out=dst[32 * q:32 * q + 4, :, :].bitcast(I32), in_=src.bitcast(I32))
 
         def load_w(g, f0, width):
             w_raw[g, f0] = const.tile([P, PACK, width], BF16, name="wraw%d_%d" % (g, f0))
@@ -107,19 +99,17 @@ def tile_linear_attention_masked_keys_g6_kernel(tc, x_words, x_scales, w_key, b_
         def group_w(g, f0, shares):
             for engine, c0, c1 in shares:
                 if c0 == 0:
-                    w_grouped[g, f0] = const.tile([P, HALF, PACK], BF16, name="wgrp%d_%d" % (g, f0), align_bytes=64)
+                    w_grouped[g, f0] = const.tile([P, w_raw[g, f0].shape[2], PACK], BF16, name="wgrp%d_%d" % (g, f0), align_bytes=64)
                 interleave(engine, w_grouped[g, f0][:, c0:c1, :], w_raw[g, f0][:, :, c0:c1], G_RUN_W if engine == "gpsimd" else 4)
 
-        def quantize_w(g, f0):
-            width = w_raw[g, f0].shape[2]
-            codes = const.tile([P, width], U32, name="wcode%d_%d" % (g, f0), align_bytes=64)
-            scales = const.tile([P, width], U8, name="wscale%d_%d" % (g, f0), align_bytes=64)
+        def quantize_w(g, f0, c0, c1):
+            codes = const.tile([P, c1 - c0], U32, name="wcode%d_%d" % (g, f0 + c0), align_bytes=64)
+            scales = const.tile([P, c1 - c0], U8, name="wscale%d_%d" % (g, f0 + c0), align_bytes=64)
             nc.vector.quantize_mx(out=codes[:].bitcast(FP8X4), scales=scales[:],
-                                  in_=w_grouped[g, f0][:].rearrange("p f t -> p (f t)"))
-            w_whole[g, f0] = (codes[:], scales[:])
-            for c in range(0, width, P):
-                w_codes[g, (f0 + c) // P] = codes[:, c:c + P]
-                w_scales[g, (f0 + c) // P] = scales[:, c:c + P]
+                                  in_=w_grouped[g, f0][:, c0:c1, :].rearrange("p f t -> p (f t)"))
+            for c in range(0, c1 - c0, P):
+                w_codes[g, (f0 + c0 + c) // P] = codes[:, c:c + P]
+                w_scales[g, (f0 + c0 + c) // P] = scales[:, c:c + P]
 
         acc = {}
         clamped = {}
@@ -140,10 +130,7 @@ def tile_linear_attention_masked_keys_g6_kernel(tc, x_words, x_scales, w_key, b_
             for g in passes:
                 if g == 0:
                     acc[n] = psum.tile([P, GROUP], F32, name="acc", bufs=MX_BANKS)
-                if grp == 0:
-                    xs = xs_first[:, g, :]
-                else:
-                    xs = xs_rest[:, g, (grp - 1) * GROUP:grp * GROUP]
+                xs = x_planes[4 * g:P, grp * GROUP:(grp + 1) * GROUP]
                 nc.tensor.matmul_mx(out=acc[n][:], lhsT=w_codes[g, ft].bitcast(FP8X4), lhsT_scale=w_scales[g, ft],
                                     rhs=x_sb[grp, g].bitcast(FP8X4), rhs_scale=xs,
                                     start=(g == 0), stop=(g == PASSES - 1))
@@ -218,21 +205,26 @@ def tile_linear_attention_masked_keys_g6_kernel(tc, x_words, x_scales, w_key, b_
                 queue.dma_start(out=out_2[:, 4 * q:4 * q + 4, c0:c1].bitcast(I32),
                                     in_=y_scales[32 * q:32 * q + 8, c0:c1].bitcast(I32))
 
-        nc.vector.memset(xs_first[:].rearrange("p g n -> p (g n)").bitcast(I32), 0)
+        make_identity(nc, ident[:])
+        nc.vector.memset(x_planes[:].bitcast(I32), 0)
+        for q in range(4):
+            nc.gpsimd.dma_start(out=x_planes[32 * q:32 * q + 4 * PASSES, :].bitcast(I32),
+                                in_=x_scales[:, 4 * q:4 * q + 4, :].bitcast(I32))
         nc.vector.memset(warm[:], 0.0)
         nc.vector.memset(b_stage[:], 0.0)
-        nc.vector.memset(xs_rest[:].rearrange("p g n -> p (g n)").bitcast(I32), 0)
-        nc.gpsimd.dma_start(out=b_rows[:], in_=b_key.rearrange("(i p) -> i p", p=P))
-        make_identity(nc, ident[:])
-        nc.gpsimd.dma_start(out=keep_raw[:], in_=keep.rearrange("j (g p t) -> p (j g) t", p=P, t=PACK))
+        nc.scalar.dma_start(out=b_rows[:], in_=b_key.rearrange("(i p) -> i p", p=P))
+        nc.scalar.dma_start(out=keep_raw[:], in_=keep.rearrange("j (g p t) -> p (j g) t", p=P, t=PACK))
         nc.scalar.activation(out=warm_out[:], in_=warm[:], func=ACT.Exp)
         load_w(0, 0, HALF)
-        load_x_scales(nc.sync, xs_first, 0, GROUP)
         load_w(1, 0, HALF)
-        load_w(2, 0, HALF)
-        for g in range(PASSES):
-            load_x(0, g, g + 1)
-        load_x_scales(nc.sync, xs_rest, GROUP, GROUPS * GROUP)
+        if ORDER == 0:
+            load_x(0, 0, 1)
+            load_w(2, 0, HALF)
+        else:
+            load_w(2, 0, HALF)
+            load_x(0, 0, 1)
+        load_x(0, 1, 2)
+        load_x(0, 2, 3)
         load_x(1, 0, PASSES)
         for g in range(PASSES):
             load_w(g, HALF, HALF)
@@ -240,85 +232,124 @@ def tile_linear_attention_masked_keys_g6_kernel(tc, x_words, x_scales, w_key, b_
         load_x(3, 0, PASSES)
 
         for g in range(PASSES):
-            group_w(g, 0, [("scalar", 0, HEAD_SPLIT), ("vector", HEAD_SPLIT, HALF)])
+            group_w(g, 0, [("vector", 0, HEAD_SPLIT), ("scalar", HEAD_SPLIT, HALF)])
             if g == 0:
+                nc.vector.tensor_copy(out=keep_col[:], in_=keep_raw[:])
+            else:
+                quantize_w(g - 1, 0, HALF // 2, HALF)
+            quantize_w(g, 0, 0, HALF // 2)
+            if g == B_AT:
                 nc.scalar.copy(out=b_stage[0:F // P, :], in_=b_rows[:])
                 b_turned = psum.tile([P, PACK, P], F32, name="turned", bufs=8 - MX_BANKS)
                 nc.tensor.transpose(b_turned[:, 0, :], b_stage[:], ident[:])
-            if g == 1:
-                nc.vector.tensor_copy(out=b_col[:], in_=b_turned[:, 0, 0:F // P])
-                nc.vector.tensor_scalar(out=b_neg[:], in0=b_turned[:, 0, 0:F // P], scalar1=-1.0, scalar2=None, op0=ALU.mult)
-                nc.vector.tensor_scalar(out=b_one[:], in0=b_turned[:, 0, 0:F // P], scalar1=1.0, scalar2=None, op0=ALU.add)
-            if g == 2:
-                nc.vector.tensor_copy(out=keep_col[:], in_=keep_raw[:])
-            quantize_w(g, 0)
-            if g == 0:
-                for rep in range(WARM):
-                    idle = psum.tile([P, GROUP], F32, name="acc", bufs=MX_BANKS)
-                    nc.tensor.matmul_mx(out=idle[:], lhsT=w_codes[0, 0].bitcast(FP8X4), lhsT_scale=w_scales[0, 0],
-                                        rhs=w_whole[0, 0][0].bitcast(FP8X4), rhs_scale=w_whole[0, 0][1], start=True, stop=True)
-        for g in range(PASSES):
             for n in range(HEAD_TILES):
                 project(n, [g])
+        nc.vector.tensor_copy(out=b_col[:], in_=b_turned[:, 0, 0:F // P])
+        nc.vector.tensor_scalar(out=b_neg[:], in0=b_turned[:, 0, 0:F // P], scalar1=-1.0, scalar2=None, op0=ALU.mult)
+        nc.vector.tensor_scalar(out=b_one[:], in0=b_turned[:, 0, 0:F // P], scalar1=1.0, scalar2=None, op0=ALU.add)
+        quantize_w(PASSES - 1, 0, HALF // 2, HALF)
 
         steps = UNITS * TILES
         last_unit = steps - TILES
-        turned_upto = [0]
-        masked_upto = [0]
 
-        for n in range(steps + 16):
-            if HEAD_TILES <= n < steps:
+        def finish(k):
+            if k % TILES == TILES - 1 and TILES <= k:
+                quantize_y(k + 1 - 2 * TILES, TILES)
+            for g in range(PASSES):
+                if k == WQ_AT[g]:
+                    quantize_w(g, HALF, 0, HALF)
+            if k == last_unit - 1:
+                store_scales(nc.sync, 0, B * F - HALF)
+            mask(k, "scalar" if k in MASK_S else "vector")
+            run = TILES if k < PAIRS_FROM else 2
+            if k % run == run - 1:
+                store_y(k + 1 - run, run)
+            if k % TILES == TILES - 1:
+                group_y(k + 1 - TILES, TILES, 0, HALF, GY)
+
+        for n in range(steps):
+            if HEAD_TILES <= n:
                 project(n, range(PASSES))
-            m = n - TURN_LAG if n < steps else min(n - MAP_LAG - 1, steps - 1)
-            if m >= turned_upto[0] and ((m + 1) % RUN == 0 or n >= steps) and m - masked_upto[0] < 8 - MX_BANKS:
-                for k in range(turned_upto[0], m + 1):
+            m = n - TURN_LAG
+            if m >= 0 and (m + 1 - RUN_AT) % RUN == 0:
+                for k in range(max(0, m + 1 - RUN), m + 1):
                     turn(k)
-                turned_upto[0] = m + 1
-            if n < steps:
-                clamp(n)
-            if EXP_LAG <= n < steps + EXP_LAG:
-                exponential(n - EXP_LAG)
-            if MAP_LAG <= n < steps + MAP_LAG:
+            clamp(n)
+            exponential(n)
+            if MAP_LAG <= n:
                 feature_map(n - MAP_LAG)
-            if n == 0:
-                group_w(1, HALF, [("gpsimd", 0, HALF)])
-                group_w(2, HALF, [("gpsimd", 0, HALF)])
-            if n == W_AT:
-                group_w(0, HALF, [("scalar", 0, HALF // 2)])
-            if n == W_AT + 1:
-                group_w(0, HALF, [("scalar", HALF // 2, HALF)])
-            for rep in range(1 if n < steps else 2):
-                k = masked_upto[0]
-                if k < turned_upto[0] and (k <= n - MASK_LAG or n >= steps):
-                    if k % TILES == TILES - 1 and TILES <= k < last_unit:
-                        quantize_y(k + 1 - 2 * TILES, TILES)
-                        for g in range(PASSES):
-                            if k == WQ_AT[g]:
-                                quantize_w(g, HALF)
-                        if k == last_unit - 1:
-                            store_scales(nc.sync, 0, B * F - HALF)
-                    if k == LAST_Q:
-                        quantize_y(last_unit - TILES, TILES)
-                    if k == steps - 1:
-                        quantize_y(last_unit, 2)
-                    mask(k, "scalar" if k % MASK_MOD == MASK_AT or k in MASK_S else "vector")
-                    masked_upto[0] = k + 1
-                    if k < last_unit:
-                        run = TILES if k < PAIRS_FROM else 2
-                        if k % run == run - 1:
-                            store_y(k + 1 - run, run)
-                        if k % TILES == TILES - 1:
-                            group_y(k + 1 - TILES, TILES, 0, HALF, GY)
-                    elif k < steps - 1:
-                        if k == last_unit + 1:
-                            store_y(k - 1, 2)
-                        if k == last_unit + 2:
-                            store_y(k, 1)
-                        group_y(k - k % 2, 2, k % 2 * P, (k % 2 + 1) * P, "scalar")
-                    else:
-                        store_y(k, 1)
-                        group_y(k - 1, 2, P, P + TAIL_SPLIT, "scalar")
-                        group_y(k - 1, 2, P + TAIL_SPLIT, 2 * P, "vector")
-                        quantize_y(k - 1, 2)
-        assert masked_upto[0] == steps
+            for engine, g, c0, c1, at in W_PLAN:
+                if n == at:
+                    group_w(g, HALF, [(engine, c0, c1)])
+            if n >= MASK_LAG:
+                finish(n - MASK_LAG)
+
+        a, b, c, d = range(last_unit, steps)
+        for k in range(steps - TURN_LAG - (steps - TURN_LAG - RUN_AT) % RUN, last_unit):
+            turn(k)
+        for k in range(steps - MASK_LAG, last_unit):
+            finish(k)
+        turn(a)
+        turn(b)
+        feature_map(c)
+        turn(c)
+        if TAIL == 0:
+            feature_map(d)
+            mask(a, "vector")
+            turn(d)
+            mask(b, "scalar")
+            store_y(a, 2)
+            mask(c, "vector")
+            group_y(a, 2, 0, 2 * P, "scalar")
+            mask(d, "vector")
+            store_y(c, 2)
+            quantize_y(last_unit - TILES, TILES)
+            group_y(c, 2, 0, TAIL_SPLIT, "scalar")
+            group_y(c, 2, TAIL_SPLIT, 2 * P, "vector")
+            quantize_y(a, 2)
+            quantize_y(c, 2)
+        if TAIL == 1:
+            feature_map(d)
+            mask(a, "vector")
+            turn(d)
+            mask(b, "scalar")
+            store_y(a, 2)
+            mask(c, "vector")
+            group_y(a, 4, 0, 2 * P, "scalar")
+            mask(d, "vector")
+            store_y(c, 2)
+            quantize_y(last_unit - TILES, TILES)
+            group_y(a, 4, 2 * P, 2 * P + TAIL_SPLIT, "scalar")
+            group_y(a, 4, 2 * P + TAIL_SPLIT, 4 * P, "vector")
+            quantize_y(a, 4)
+        if TAIL == 2:
+            mask(a, "vector")
+            feature_map(d)
+            turn(d)
+            mask(b, "vector")
+            group_y(a, 2, 0, P, "scalar")
+            store_y(a, 2)
+            mask(c, "scalar")
+            mask(d, "vector")
+            group_y(a, 2, P, 2 * P, "scalar")
+            store_y(c, 2)
+            quantize_y(last_unit - TILES, TILES)
+            group_y(c, 2, 0, TAIL_SPLIT, "scalar")
+            group_y(c, 2, TAIL_SPLIT, 2 * P, "vector")
+            quantize_y(a, 2)
+            quantize_y(c, 2)
+        if TAIL == 3:
+            feature_map(d)
+            mask(a, "scalar")
+            turn(d)
+            mask(b, "vector")
+            store_y(a, 2)
+            mask(c, "scalar")
+            mask(d, "vector")
+            store_y(c, 2)
+            group_y(a, 2, 0, 2 * P, "scalar")
+            quantize_y(last_unit - TILES, TILES)
+            group_y(c, 2, 0, 2 * P, "vector")
+            quantize_y(a, 2)
+            quantize_y(c, 2)
         store_scales(nc.scalar, B * F - HALF, B * F)

@@ -24,24 +24,25 @@ HALF = 512
 HALVES = F // HALF
 TILES = HALF // P
 UNITS = GROUPS * HALVES
-MX_BANKS = 4
+MX_BANKS = 5
 RUN = 2
 TURN_LAG = 3
 MASK_LAG = 4
 HEAD_V = 6
-WQ_AT = (7, 7, 7)
+WQ_AT = (3, 7)
 PAIRS_FROM = 24
-W_PLAN = (("gpsimd", 0, 0, 512, 0), ("gpsimd", 1, 0, 512, 0), ("scalar", 2, 0, 256, 4), ("scalar", 2, 256, 512, 5))
-MASK_S = (9, 21)
+MASK_S = ()
 TAIL_SPLIT = 96
 TAIL = 3
 RUN_AT = 0
+W2_AT = 5
+EARLY_Q = 3
+EXP_LAG = 1
 HEAD_TILES = 2
 MAP_LAG = 2
 HEAD_SPLIT = 320
 ORDER = 0
 B_AT = 1
-YG_BUFS = 4
 GY = "gpsimd"
 G_RUN_W = 1
 G_RUN_Y = 1
@@ -99,7 +100,7 @@ def tile_linear_attention_masked_keys_g6_kernel(tc, x_words, x_scales, w_key, b_
         def group_w(g, f0, shares):
             for engine, c0, c1 in shares:
                 if c0 == 0:
-                    w_grouped[g, f0] = const.tile([P, w_raw[g, f0].shape[2], PACK], BF16, name="wgrp%d_%d" % (g, f0), align_bytes=64)
+                    w_grouped[g, f0] = const.tile([P, HALF, PACK], BF16, name="wgrp_late" if engine == "gpsimd" else "wgrp%d_%d" % (g, f0), align_bytes=64)
                 interleave(engine, w_grouped[g, f0][:, c0:c1, :], w_raw[g, f0][:, :, c0:c1], G_RUN_W if engine == "gpsimd" else 4)
 
         def quantize_w(g, f0, c0, c1):
@@ -184,10 +185,10 @@ def tile_linear_attention_masked_keys_g6_kernel(tc, x_words, x_scales, w_key, b_
             dst = out_0[j, g * GROUP:(g + 1) * GROUP, f0:f0 + count * P].rearrange("(p t) f -> p t f", t=PACK)
             nc.sync.dma_start(out=dst, in_=y[n // TILES][:, :, i * P:(i + count) * P])
 
-        def group_y(n, count, c0, c1, engine):
+        def group_y(n, count, c0, c1, engine, tag="y_last", bufs=2):
             i = n % TILES
             if c0 == 0:
-                y_grouped[n] = work.tile([P, count * P, PACK], BF16, name="y_grouped", bufs=YG_BUFS, align_bytes=64)
+                y_grouped[n] = work.tile([P, count * P, PACK], BF16, name=tag, bufs=bufs, align_bytes=64)
             interleave(engine, y_grouped[n][:, c0:c1, :], y[n // TILES][:, :, i * P + c0:i * P + c1], G_RUN_Y if engine == "gpsimd" else 2)
 
         def quantize_y(n, count):
@@ -200,22 +201,22 @@ def tile_linear_attention_masked_keys_g6_kernel(tc, x_words, x_scales, w_key, b_
             dst = out_1[g, :, c0:c0 + count * P, :].rearrange("p m t -> p (m t)")
             nc.sync.dma_start(out=dst.bitcast(I32), in_=codes[:].bitcast(I32))
 
-        def store_scales(queue, c0, c1):
+        def store_scales(even, odd, c0, c1):
             for q in range(4):
+                queue = odd if q % 2 else even
                 queue.dma_start(out=out_2[:, 4 * q:4 * q + 4, c0:c1].bitcast(I32),
                                     in_=y_scales[32 * q:32 * q + 8, c0:c1].bitcast(I32))
 
-        make_identity(nc, ident[:])
         nc.vector.memset(x_planes[:].bitcast(I32), 0)
+        nc.vector.memset(warm[:], 0.0)
+        nc.vector.memset(b_stage[:], 0.0)
         for q in range(4):
             nc.gpsimd.dma_start(out=x_planes[32 * q:32 * q + 4 * PASSES, :].bitcast(I32),
                                 in_=x_scales[:, 4 * q:4 * q + 4, :].bitcast(I32))
-        nc.vector.memset(warm[:], 0.0)
-        nc.vector.memset(b_stage[:], 0.0)
-        nc.scalar.dma_start(out=b_rows[:], in_=b_key.rearrange("(i p) -> i p", p=P))
-        nc.scalar.dma_start(out=keep_raw[:], in_=keep.rearrange("j (g p t) -> p (j g) t", p=P, t=PACK))
+        make_identity(nc, ident[:])
         nc.scalar.activation(out=warm_out[:], in_=warm[:], func=ACT.Exp)
         load_w(0, 0, HALF)
+        nc.sync.dma_start(out=b_rows[:], in_=b_key.rearrange("(i p) -> i p", p=P))
         load_w(1, 0, HALF)
         if ORDER == 0:
             load_x(0, 0, 1)
@@ -225,17 +226,17 @@ def tile_linear_attention_masked_keys_g6_kernel(tc, x_words, x_scales, w_key, b_
             load_x(0, 0, 1)
         load_x(0, 1, 2)
         load_x(0, 2, 3)
+        load_w(0, HALF, HALF)
         load_x(1, 0, PASSES)
-        for g in range(PASSES):
-            load_w(g, HALF, HALF)
+        load_w(1, HALF, HALF)
+        nc.sync.dma_start(out=keep_raw[:], in_=keep.rearrange("j (g p t) -> p (j g) t", p=P, t=PACK))
+        load_w(2, HALF, HALF)
         load_x(2, 0, PASSES)
         load_x(3, 0, PASSES)
 
         for g in range(PASSES):
             group_w(g, 0, [("vector", 0, HEAD_SPLIT), ("scalar", HEAD_SPLIT, HALF)])
-            if g == 0:
-                nc.vector.tensor_copy(out=keep_col[:], in_=keep_raw[:])
-            else:
+            if g > 0:
                 quantize_w(g - 1, 0, HALF // 2, HALF)
             quantize_w(g, 0, 0, HALF // 2)
             if g == B_AT:
@@ -253,19 +254,20 @@ def tile_linear_attention_masked_keys_g6_kernel(tc, x_words, x_scales, w_key, b_
         last_unit = steps - TILES
 
         def finish(k):
-            if k % TILES == TILES - 1 and TILES <= k:
-                quantize_y(k + 1 - 2 * TILES, TILES)
-            for g in range(PASSES):
-                if k == WQ_AT[g]:
-                    quantize_w(g, HALF, 0, HALF)
-            if k == last_unit - 1:
-                store_scales(nc.sync, 0, B * F - HALF)
+            first = k - k % TILES
+            if TILES <= first and k - first == (TILES - 1 if first < PAIRS_FROM else EARLY_Q):
+                quantize_y(first - TILES, TILES)
+                if first == TILES:
+                    quantize_w(PASSES - 1, HALF, 0, HALF)
+                if first == last_unit - TILES:
+                    store_scales(nc.sync, nc.sync, 0, B * F - HALF)
+                    group_y(first, TILES, 0, 2 * P, GY, "y_grouped", 1)
             mask(k, "scalar" if k in MASK_S else "vector")
             run = TILES if k < PAIRS_FROM else 2
             if k % run == run - 1:
                 store_y(k + 1 - run, run)
             if k % TILES == TILES - 1:
-                group_y(k + 1 - TILES, TILES, 0, HALF, GY)
+                group_y(first, TILES, HALF - run * P, HALF, GY, "y_grouped", 1)
 
         for n in range(steps):
             if HEAD_TILES <= n:
@@ -275,16 +277,29 @@ def tile_linear_attention_masked_keys_g6_kernel(tc, x_words, x_scales, w_key, b_
                 for k in range(max(0, m + 1 - RUN), m + 1):
                     turn(k)
             clamp(n)
-            exponential(n)
+            if n >= EXP_LAG:
+                exponential(n - EXP_LAG)
             if MAP_LAG <= n:
                 feature_map(n - MAP_LAG)
-            for engine, g, c0, c1, at in W_PLAN:
-                if n == at:
-                    group_w(g, HALF, [(engine, c0, c1)])
+            if n == 0:
+                group_w(0, HALF, [("gpsimd", 0, HALF)])
+            for g in range(PASSES - 1):
+                if n == WQ_AT[g]:
+                    quantize_w(g, HALF, 0, HALF)
+                    if g == 0 or W2_AT < 0:
+                        group_w(g + 1, HALF, [("gpsimd", 0, HALF)])
+            if n == W2_AT:
+                group_w(2, HALF, [("scalar", 0, HALF // 2)])
+            if n == W2_AT + 1 and W2_AT >= 0:
+                group_w(2, HALF, [("scalar", HALF // 2, HALF)])
+            if n == MASK_LAG - 1:
+                nc.scalar.copy(out=keep_col[:], in_=keep_raw[:])
             if n >= MASK_LAG:
                 finish(n - MASK_LAG)
 
         a, b, c, d = range(last_unit, steps)
+        for k in range(steps - EXP_LAG, steps):
+            exponential(k)
         for k in range(steps - TURN_LAG - (steps - TURN_LAG - RUN_AT) % RUN, last_unit):
             turn(k)
         for k in range(steps - MASK_LAG, last_unit):
@@ -352,4 +367,4 @@ def tile_linear_attention_masked_keys_g6_kernel(tc, x_words, x_scales, w_key, b_
             group_y(c, 2, 0, 2 * P, "vector")
             quantize_y(a, 2)
             quantize_y(c, 2)
-        store_scales(nc.scalar, B * F - HALF, B * F)
+        store_scales(nc.scalar, nc.sync, B * F - HALF, B * F)

@@ -31,7 +31,7 @@ MASK_LAG = 4
 HEAD_V = 6
 WQ_AT = (3, 7)
 PAIRS_FROM = 24
-MASK_S = ()
+MASK_S = (8,)
 TAIL_SPLIT = 96
 TAIL = 3
 RUN_AT = 0
@@ -66,7 +66,8 @@ def tile_linear_attention_masked_keys_g6_kernel(tc, x_words, x_scales, w_key, b_
         keep_col = const.tile([P, GROUPS, PACK], F32, name="keep_col")
         warm = const.tile([P, 1], F32, name="warm")
         warm_out = const.tile([P, 1], F32, name="warm_out")
-        x_planes = const.tile([P, B * S], U8, name="x_planes", align_bytes=64)
+        xs_first = const.tile([P, PASSES, GROUP], U8, name="xs_first", align_bytes=64)
+        xs_rest = const.tile([P, B * S - GROUP], U8, name="xs_rest", align_bytes=64)
         y_scales = const.tile([P, B * F], U8, name="y_scales", align_bytes=64)
 
         x_sb = {}
@@ -131,7 +132,7 @@ def tile_linear_attention_masked_keys_g6_kernel(tc, x_words, x_scales, w_key, b_
             for g in passes:
                 if g == 0:
                     acc[n] = psum.tile([P, GROUP], F32, name="acc", bufs=MX_BANKS)
-                xs = x_planes[4 * g:P, grp * GROUP:(grp + 1) * GROUP]
+                xs = xs_first[:, g, :] if grp == 0 else xs_rest[4 * g:P, (grp - 1) * GROUP:grp * GROUP]
                 nc.tensor.matmul_mx(out=acc[n][:], lhsT=w_codes[g, ft].bitcast(FP8X4), lhsT_scale=w_scales[g, ft],
                                     rhs=x_sb[grp, g].bitcast(FP8X4), rhs_scale=xs,
                                     start=(g == 0), stop=(g == PASSES - 1))
@@ -139,15 +140,21 @@ def tile_linear_attention_masked_keys_g6_kernel(tc, x_words, x_scales, w_key, b_
         def by_slot(n):
             return acc[n][:].rearrange("p (m t) -> p t m", t=PACK)
 
+        def in_runs_of(n):
+            return acc[n][:].rearrange("p (c i t) -> p c t i", i=4, t=PACK)
+
+        def in_runs(slots):
+            return slots[:].rearrange("p t (c i) -> p c t i", i=4)
+
         def clamp(n):
             grp, half, i = place(n)
             ft = half * TILES + i
             clamped[n] = work.tile([P, PACK, P], F32, name="clamped", bufs=3)
             if n < HEAD_V:
-                nc.vector.tensor_scalar(out=clamped[n][:], in0=by_slot(n), scalar1=b_col[:, ft:ft + 1], scalar2=0.0,
+                nc.vector.tensor_scalar(out=in_runs(clamped[n]), in0=in_runs_of(n), scalar1=b_col[:, ft:ft + 1], scalar2=0.0,
                                         op0=ALU.add, op1=ALU.min)
             else:
-                nc.scalar.activation(out=clamped[n][:], in_=by_slot(n), func=ACT.Relu, bias=b_neg[:, ft:ft + 1], scale=-1.0)
+                nc.scalar.activation(out=in_runs(clamped[n]), in_=in_runs_of(n), func=ACT.Relu, bias=b_neg[:, ft:ft + 1], scale=-1.0)
 
         def exponential(n):
             expo[n] = work.tile([P, PACK, P], F32, name="expo", bufs=3)
@@ -207,16 +214,20 @@ def tile_linear_attention_masked_keys_g6_kernel(tc, x_words, x_scales, w_key, b_
                 queue.dma_start(out=out_2[:, 4 * q:4 * q + 4, c0:c1].bitcast(I32),
                                     in_=y_scales[32 * q:32 * q + 8, c0:c1].bitcast(I32))
 
-        nc.vector.memset(x_planes[:].bitcast(I32), 0)
+        nc.vector.memset(xs_first[:].rearrange("p g n -> p (g n)").bitcast(I32), 0)
         nc.vector.memset(warm[:], 0.0)
         nc.vector.memset(b_stage[:], 0.0)
-        for q in range(4):
-            nc.gpsimd.dma_start(out=x_planes[32 * q:32 * q + 4 * PASSES, :].bitcast(I32),
-                                in_=x_scales[:, 4 * q:4 * q + 4, :].bitcast(I32))
+        nc.vector.memset(xs_rest[:].bitcast(I32), 0)
         make_identity(nc, ident[:])
+        for q in range(4):
+            nc.gpsimd.dma_start(out=xs_rest[32 * q:32 * q + 4 * PASSES, :].bitcast(I32),
+                                in_=x_scales[:, 4 * q:4 * q + 4, GROUP:].bitcast(I32))
         nc.scalar.activation(out=warm_out[:], in_=warm[:], func=ACT.Exp)
         load_w(0, 0, HALF)
         nc.sync.dma_start(out=b_rows[:], in_=b_key.rearrange("(i p) -> i p", p=P))
+        for q in range(4):
+            src = x_scales[:, 4 * q:4 * q + 4, 0:GROUP].rearrange("g r n -> r g n")
+            nc.sync.dma_start(out=xs_first[32 * q:32 * q + 4, :, :].bitcast(I32), in_=src.bitcast(I32))
         load_w(1, 0, HALF)
         if ORDER == 0:
             load_x(0, 0, 1)

from contextlib import ExitStack

import concourse.mybir as mybir
from concourse.masks import make_identity

B, S, D, F = 2, 1024, 1536, 1024
FLOPS = 2 * B * S * D * F

F32 = mybir.dt.float32
BF16 = mybir.dt.bfloat16
I32 = mybir.dt.int32
U32 = mybir.dt.uint32
U8 = mybir.dt.uint8
FP8X4 = mybir.dt.float8_e4m3fn_x4
ALU = mybir.AluOpType
ACT = mybir.ActivationFunctionType

P = 128
PACK = 4
GROUP = P * PACK
PASSES = D // GROUP
GROUPS = B * S // GROUP
HALF = 512
HALVES = F // HALF
TILES = HALF // P
UNITS = GROUPS * HALVES
MX_BANKS = 5
RUN = 2
TURN_LAG = 3
MASK_LAG = 4
HEAD_V = 6
WQ_AT = (3, 7)
PAIRS_FROM = 24
MASK_S = (8,)
TAIL_SPLIT = 96
TAIL = 3
RUN_AT = 0
W2_AT = 5
EARLY_Q = 3
EXP_LAG = 1
HEAD_TILES = 2
MAP_LAG = 2
HEAD_SPLIT = 320
ORDER = 0
B_AT = 1
GY = "gpsimd"
G_RUN_W = 1
G_RUN_Y = 1


def tile_linear_attention_masked_keys_g6_kernel(tc, x_words, x_scales, w_key, b_key, keep, out_0, out_1, out_2):
    nc = tc.nc
    with ExitStack() as ctx:
        const = ctx.enter_context(tc.tile_pool(name="const", bufs=1))
        work = ctx.enter_context(tc.tile_pool(name="work", bufs=1))
        psum = ctx.enter_context(tc.psum_pool(name="psum", bufs=1))
        ctx.enter_context(tc.manual_schedule())

        ident = const.tile([P, P], F32, name="ident")
        b_rows = const.tile([F // P, P], BF16, name="b_rows")
        b_stage = const.tile([P, P], F32, name="b_stage")
        b_col = const.tile([P, F // P], F32, name="b_col")
        b_neg = const.tile([P, F // P], F32, name="b_neg")
        b_one = const.tile([P, F // P], F32, name="b_one")
        keep_raw = const.tile([P, GROUPS, PACK], BF16, name="keep_raw")
        keep_col = const.tile([P, GROUPS, PACK], F32, name="keep_col")
        warm = const.tile([P, 1], F32, name="warm")
        warm_out = const.tile([P, 1], F32, name="warm_out")
        xs_first = const.tile([P, PASSES, GROUP], U8, name="xs_first", align_bytes=64)
        xs_rest = const.tile([P, B * S - GROUP], U8, name="xs_rest", align_bytes=64)
        y_scales = const.tile([P, B * F], U8, name="y_scales", align_bytes=64)

        x_sb = {}
        w_raw = {}
        w_grouped = {}
        w_codes = {}
        w_scales = {}

        def load_x(grp, g0, g1):
            words = const.tile([P, g1 - g0, GROUP], U32, name="x%d_%d" % (grp, g0), align_bytes=64)
            src = x_words[g0:g1, :, grp * GROUP:(grp + 1) * GROUP, :].rearrange("g p n t -> p g (n t)")
            nc.sync.dma_start(out=words[:].bitcast(I32), in_=src.bitcast(I32))
            for g in range(g0, g1):
                x_sb[grp, g] = words[:, g - g0, :]

        def load_w(g, f0, width):
            w_raw[g, f0] = const.tile([P, PACK, width], BF16, name="wraw%d_%d" % (g, f0))
            src = w_key[g * GROUP:(g + 1) * GROUP, f0:f0 + width].rearrange("(p j) f -> p j f", j=PACK)
            nc.sync.dma_start(out=w_raw[g, f0][:], in_=src)

        def interleave(engine, dst, src, run):
            dst_v = dst.rearrange("p (c i) t -> p c t i", i=run)
            src_v = src.rearrange("p t (c i) -> p c t i", i=run)
            if engine == "gpsimd":
                nc.gpsimd.tensor_scalar(out=dst_v, in0=src_v, scalar1=1.0, scalar2=0.0, op0=ALU.mult, op1=ALU.add)
            elif engine == "scalar":
                nc.scalar.copy(out=dst_v, in_=src_v)
            else:
                nc.vector.tensor_copy(out=dst_v, in_=src_v)

        def group_w(g, f0, shares):
            for engine, c0, c1 in shares:
                if c0 == 0:
                    w_grouped[g, f0] = const.tile([P, HALF, PACK], BF16, name="wgrp_late" if engine == "gpsimd" else "wgrp%d_%d" % (g, f0), align_bytes=64)
                interleave(engine, w_grouped[g, f0][:, c0:c1, :], w_raw[g, f0][:, :, c0:c1], G_RUN_W if engine == "gpsimd" else 4)

        def quantize_w(g, f0, c0, c1):
            codes = const.tile([P, c1 - c0], U32, name="wcode%d_%d" % (g, f0 + c0), align_bytes=64)
            scales = const.tile([P, c1 - c0], U8, name="wscale%d_%d" % (g, f0 + c0), align_bytes=64)
            nc.vector.quantize_mx(out=codes[:].bitcast(FP8X4), scales=scales[:],
                                  in_=w_grouped[g, f0][:, c0:c1, :].rearrange("p f t -> p (f t)"))
            for c in range(0, c1 - c0, P):
                w_codes[g, (f0 + c0 + c) // P] = codes[:, c:c + P]
                w_scales[g, (f0 + c0 + c) // P] = scales[:, c:c + P]

        acc = {}
        clamped = {}
        expo = {}
        phi = {}
        turned = {}
        y = {}
        y_grouped = {}

        def place(n):
            u, i = divmod(n, TILES)
            grp, half = u % GROUPS, u // GROUPS
            return grp, half, i

        def project(n, passes):
            grp, half, i = place(n)
            ft = half * TILES + i
            for g in passes:
                if g == 0:
                    acc[n] = psum.tile([P, GROUP], F32, name="acc", bufs=MX_BANKS)
                xs = xs_first[:, g, :] if grp == 0 else xs_rest[4 * g:P, (grp - 1) * GROUP:grp * GROUP]
                nc.tensor.matmul_mx(out=acc[n][:], lhsT=w_codes[g, ft].bitcast(FP8X4), lhsT_scale=w_scales[g, ft],
                                    rhs=x_sb[grp, g].bitcast(FP8X4), rhs_scale=xs,
                                    start=(g == 0), stop=(g == PASSES - 1))

        def by_slot(n):
            return acc[n][:].rearrange("p (m t) -> p t m", t=PACK)

        def in_runs_of(n):
            return acc[n][:].rearrange("p (c i t) -> p c t i", i=4, t=PACK)

        def in_runs(slots):
            return slots[:].rearrange("p t (c i) -> p c t i", i=4)

        def clamp(n):
            grp, half, i = place(n)
            ft = half * TILES + i
            clamped[n] = work.tile([P, PACK, P], F32, name="clamped", bufs=3)
            if n < HEAD_V:
                nc.vector.tensor_scalar(out=in_runs(clamped[n]), in0=in_runs_of(n), scalar1=b_col[:, ft:ft + 1], scalar2=0.0,
                                        op0=ALU.add, op1=ALU.min)
            else:
                nc.scalar.activation(out=in_runs(clamped[n]), in_=in_runs_of(n), func=ACT.Relu, bias=b_neg[:, ft:ft + 1], scale=-1.0)

        def exponential(n):
            expo[n] = work.tile([P, PACK, P], F32, name="expo", bufs=3)
            nc.scalar.activation(out=expo[n][:], in_=clamped[n][:], func=ACT.Exp, scale=1.0 if n < HEAD_V else -1.0)

        def feature_map(n):
            grp, half, i = place(n)
            ft = half * TILES + i
            phi[n] = work.tile([P, PACK, P], F32, name="phi", bufs=10)
            nc.vector.scalar_tensor_tensor(out=phi[n][:], in0=by_slot(n), scalar=b_one[:, ft:ft + 1], in1=expo[n][:],
                                           op0=ALU.add, op1=ALU.max)

        def turn(n):
            turned[n] = psum.tile([P, PACK, P], F32, name="turned", bufs=8 - MX_BANKS)
            for t in range(PACK):
                nc.tensor.transpose(turned[n][:, t, :], phi[n][:, t, :], ident[:])

        def mask(n, engine):
            grp, half, i = place(n)
            u = n // TILES
            if i == 0:
                y[u] = work.tile([P, PACK, HALF], F32, name="y", bufs=3)
            cols = slice(i * P, (i + 1) * P)
            if engine == "scalar":
                for t in range(PACK):
                    nc.scalar.activation(out=y[u][:, t, cols], in_=turned[n][:, t, :], func=ACT.Copy, scale=keep_col[:, grp, t:t + 1])
            else:
                nc.vector.tensor_tensor(out=y[u][:, :, cols], in0=turned[n][:],
                                        in1=keep_col[:, grp, :].unsqueeze(2).to_broadcast([P, PACK, P]), op=ALU.mult)

        def store_y(n, count):
            grp, half, i = place(n)
            j, g = divmod(grp, S // GROUP)
            f0 = half * HALF + i * P
            dst = out_0[j, g * GROUP:(g + 1) * GROUP, f0:f0 + count * P].rearrange("(p t) f -> p t f", t=PACK)
            nc.sync.dma_start(out=dst, in_=y[n // TILES][:, :, i * P:(i + count) * P])

        def group_y(n, count, c0, c1, engine, tag="y_last", bufs=2):
            i = n % TILES
            if c0 == 0:
                y_grouped[n] = work.tile([P, count * P, PACK], BF16, name=tag, bufs=bufs, align_bytes=64)
            interleave(engine, y_grouped[n][:, c0:c1, :], y[n // TILES][:, :, i * P + c0:i * P + c1], G_RUN_Y if engine == "gpsimd" else 2)

        def quantize_y(n, count):
            grp, half, i = place(n)
            j, g = divmod(grp, S // GROUP)
            c0 = j * F + half * HALF + i * P
            codes = work.tile([P, count * P], U32, name="y_codes", bufs=4, align_bytes=64)
            nc.vector.quantize_mx(out=codes[:].bitcast(FP8X4), scales=y_scales[4 * g:P, c0:c0 + count * P],
                                  in_=y_grouped[n][:].rearrange("p f t -> p (f t)"))
            dst = out_1[g, :, c0:c0 + count * P, :].rearrange("p m t -> p (m t)")
            nc.sync.dma_start(out=dst.bitcast(I32), in_=codes[:].bitcast(I32))

        def store_scales(even, odd, c0, c1):
            for q in range(4):
                queue = odd if q % 2 else even
                queue.dma_start(out=out_2[:, 4 * q:4 * q + 4, c0:c1].bitcast(I32),
                                    in_=y_scales[32 * q:32 * q + 8, c0:c1].bitcast(I32))

        nc.vector.memset(xs_first[:].rearrange("p g n -> p (g n)").bitcast(I32), 0)
        nc.vector.memset(warm[:], 0.0)
        nc.vector.memset(b_stage[:], 0.0)
        nc.vector.memset(xs_rest[:].bitcast(I32), 0)
        make_identity(nc, ident[:])
        for q in range(4):
            nc.gpsimd.dma_start(out=xs_rest[32 * q:32 * q + 4 * PASSES, :].bitcast(I32),
                                in_=x_scales[:, 4 * q:4 * q + 4, GROUP:].bitcast(I32))
        nc.scalar.activation(out=warm_out[:], in_=warm[:], func=ACT.Exp)
        load_w(0, 0, HALF)
        nc.sync.dma_start(out=b_rows[:], in_=b_key.rearrange("(i p) -> i p", p=P))
        for q in range(4):
            src = x_scales[:, 4 * q:4 * q + 4, 0:GROUP].rearrange("g r n -> r g n")
            nc.sync.dma_start(out=xs_first[32 * q:32 * q + 4, :, :].bitcast(I32), in_=src.bitcast(I32))
        load_w(1, 0, HALF)
        if ORDER == 0:
            load_x(0, 0, 1)
            load_w(2, 0, HALF)
        else:
            load_w(2, 0, HALF)
            load_x(0, 0, 1)
        load_x(0, 1, 2)
        load_x(0, 2, 3)
        load_w(0, HALF, HALF)
        load_x(1, 0, PASSES)
        load_w(1, HALF, HALF)
        nc.sync.dma_start(out=keep_raw[:], in_=keep.rearrange("j (g p t) -> p (j g) t", p=P, t=PACK))
        load_w(2, HALF, HALF)
        load_x(2, 0, PASSES)
        load_x(3, 0, PASSES)

        for g in range(PASSES):
            group_w(g, 0, [("vector", 0, HEAD_SPLIT), ("scalar", HEAD_SPLIT, HALF)])
            if g > 0:
                quantize_w(g - 1, 0, HALF // 2, HALF)
            quantize_w(g, 0, 0, HALF // 2)
            if g == B_AT:
                nc.scalar.copy(out=b_stage[0:F // P, :], in_=b_rows[:])
                b_turned = psum.tile([P, PACK, P], F32, name="turned", bufs=8 - MX_BANKS)
                nc.tensor.transpose(b_turned[:, 0, :], b_stage[:], ident[:])
            for n in range(HEAD_TILES):
                project(n, [g])
        nc.vector.tensor_copy(out=b_col[:], in_=b_turned[:, 0, 0:F // P])
        nc.vector.tensor_scalar(out=b_neg[:], in0=b_turned[:, 0, 0:F // P], scalar1=-1.0, scalar2=None, op0=ALU.mult)
        nc.vector.tensor_scalar(out=b_one[:], in0=b_turned[:, 0, 0:F // P], scalar1=1.0, scalar2=None, op0=ALU.add)
        quantize_w(PASSES - 1, 0, HALF // 2, HALF)

        steps = UNITS * TILES
        last_unit = steps - TILES

        def finish(k):
            first = k - k % TILES
            if TILES <= first and k - first == (TILES - 1 if first < PAIRS_FROM else EARLY_Q):
                quantize_y(first - TILES, TILES)
                if first == TILES:
                    quantize_w(PASSES - 1, HALF, 0, HALF)
                if first == last_unit - TILES:
                    store_scales(nc.sync, nc.sync, 0, B * F - HALF)
                    group_y(first, TILES, 0, 2 * P, GY, "y_grouped", 1)
            mask(k, "scalar" if k in MASK_S else "vector")
            run = TILES if k < PAIRS_FROM else 2
            if k % run == run - 1:
                store_y(k + 1 - run, run)
            if k % TILES == TILES - 1:
                group_y(first, TILES, HALF - run * P, HALF, GY, "y_grouped", 1)

        for n in range(steps):
            if HEAD_TILES <= n:
                project(n, range(PASSES))
            m = n - TURN_LAG
            if m >= 0 and (m + 1 - RUN_AT) % RUN == 0:
                for k in range(max(0, m + 1 - RUN), m + 1):
                    turn(k)
            clamp(n)
            if n >= EXP_LAG:
                exponential(n - EXP_LAG)
            if MAP_LAG <= n:
                feature_map(n - MAP_LAG)
            if n == 0:
                group_w(0, HALF, [("gpsimd", 0, HALF)])
            for g in range(PASSES - 1):
                if n == WQ_AT[g]:
                    quantize_w(g, HALF, 0, HALF)
                    if g == 0 or W2_AT < 0:
                        group_w(g + 1, HALF, [("gpsimd", 0, HALF)])
            if n == W2_AT:
                group_w(2, HALF, [("scalar", 0, HALF // 2)])
            if n == W2_AT + 1 and W2_AT >= 0:
                group_w(2, HALF, [("scalar", HALF // 2, HALF)])
            if n == MASK_LAG - 1:
                nc.scalar.copy(out=keep_col[:], in_=keep_raw[:])
            if n >= MASK_LAG:
                finish(n - MASK_LAG)

        a, b, c, d = range(last_unit, steps)
        for k in range(steps - EXP_LAG, steps):
            exponential(k)
        for k in range(steps - TURN_LAG - (steps - TURN_LAG - RUN_AT) % RUN, last_unit):
            turn(k)
        for k in range(steps - MASK_LAG, last_unit):
            finish(k)
        turn(a)
        turn(b)
        feature_map(c)
        turn(c)
        if TAIL == 0:
            feature_map(d)
            mask(a, "vector")
            turn(d)
            mask(b, "scalar")
            store_y(a, 2)
            mask(c, "vector")
            group_y(a, 2, 0, 2 * P, "scalar")
            mask(d, "vector")
            store_y(c, 2)
            quantize_y(last_unit - TILES, TILES)
            group_y(c, 2, 0, TAIL_SPLIT, "scalar")
            group_y(c, 2, TAIL_SPLIT, 2 * P, "vector")
            quantize_y(a, 2)
            quantize_y(c, 2)
        if TAIL == 1:
            feature_map(d)
            mask(a, "vector")
            turn(d)
            mask(b, "scalar")
            store_y(a, 2)
            mask(c, "vector")
            group_y(a, 4, 0, 2 * P, "scalar")
            mask(d, "vector")
            store_y(c, 2)
            quantize_y(last_unit - TILES, TILES)
            group_y(a, 4, 2 * P, 2 * P + TAIL_SPLIT, "scalar")
            group_y(a, 4, 2 * P + TAIL_SPLIT, 4 * P, "vector")
            quantize_y(a, 4)
        if TAIL == 2:
            mask(a, "vector")
            feature_map(d)
            turn(d)
            mask(b, "vector")
            group_y(a, 2, 0, P, "scalar")
            store_y(a, 2)
            mask(c, "scalar")
            mask(d, "vector")
            group_y(a, 2, P, 2 * P, "scalar")
            store_y(c, 2)
            quantize_y(last_unit - TILES, TILES)
            group_y(c, 2, 0, TAIL_SPLIT, "scalar")
            group_y(c, 2, TAIL_SPLIT, 2 * P, "vector")
            quantize_y(a, 2)
            quantize_y(c, 2)
        if TAIL == 3:
            feature_map(d)
            mask(a, "scalar")
            turn(d)
            mask(b, "vector")
            store_y(a, 2)
            mask(c, "scalar")
            mask(d, "vector")
            store_y(c, 2)
            group_y(a, 2, 0, 2 * P, "scalar")
            quantize_y(last_unit - TILES, TILES)
            group_y(c, 2, 0, 2 * P, "vector")
            quantize_y(a, 2)
            quantize_y(c, 2)
        store_scales(nc.scalar, nc.sync, B * F - HALF, B * F)
